import numpy as np
import ml_dtypes


def mxq(x, axis, fmt="e4m3"):
    dtype, down = {"e4m3": (ml_dtypes.float8_e4m3fn, 7), "e5m2": (ml_dtypes.float8_e5m2, 14)}[fmt]
    v = np.moveaxis(np.asarray(x, np.float32).astype(ml_dtypes.bfloat16).astype(np.float64), axis, -1)
    blocks = v.reshape(v.shape[:-1] + (-1, 32))
    amax = np.abs(blocks).max(-1, keepdims=True)
    byte = np.maximum(np.where(amax > 0, np.frexp(amax)[1] - 1 + 127, 0) - down, 1)
    scale = np.exp2(byte - 127.0)
    codes = (blocks / scale).astype(np.float32).astype(dtype).astype(np.float64)
    return np.moveaxis((codes * scale).reshape(v.shape), -1, axis)


WIDE = False


def mx_kscale(k):
    if not WIDE:
        return np.ones(k)
    levels = np.array([10, -10, 5, -5, 0])
    if k % 512:
        return np.exp2(np.random.permutation(np.resize(levels, k // 32))).repeat(32)
    a = np.empty((k // 512, 16))
    for p in range(k // 512):
        a[p, :8] = np.random.permutation(np.resize(levels, 8))
        for g in range(8):
            far = levels[np.abs(levels - a[p, g]) >= 10]
            a[p, g + 8] = far[np.random.randint(len(far))]
    return np.exp2(a.ravel()).repeat(32)


def f64(x):
    return np.asarray(x).astype(np.float64)


def striped(idx):
    return np.tile(idx.reshape(-1, 16).T, (8, 1)).astype(np.uint16)


def unstriped(offs):
    return offs[:16].T.reshape(-1).astype(np.int64)


E2M1 = np.array([0.0, 0.5, 1.0, 1.5, 2.0, 3.0, 4.0, 6.0, -0.0, -0.5, -1.0, -1.5, -2.0, -3.0, -4.0, -6.0])


def pack_weight(w, fmt):
    k, n = w.shape
    w = f64(np.asarray(w, np.float32).astype(ml_dtypes.bfloat16)).reshape(k // 32, 32, n)
    amax = np.abs(w).max(1)
    if fmt == "e4m3":
        byte = np.frexp(amax)[1] - 1 + 127 - 7
    else:
        mant, ex = np.frexp(amax / 6.0)
        byte = np.where(mant > 0.5, ex, ex - 1) + 127
    byte = np.clip(np.where(amax > 0, byte, 1), 1, 254)
    scaled = (w * np.exp2(127.0 - byte)[:, None, :]).reshape(k, n).astype(np.float32)
    by_word = np.ascontiguousarray(scaled.reshape(k // 512, 128, 4, n).transpose(0, 1, 3, 2))
    if fmt == "e4m3":
        words = by_word.astype(ml_dtypes.float8_e4m3fn).view(np.uint8)
    else:
        c = by_word.astype(ml_dtypes.float4_e2m1fn).view(np.uint8) & 0xF
        words = (c[..., 0::2] | (c[..., 1::2] << 4)).reshape(k // 512, 128, 2 * n)
    return np.ascontiguousarray(words), np.ascontiguousarray(byte.astype(np.uint8).reshape(k // 512, 16, n))


def unpack_weight(words, scales, fmt):
    g, _, n = scales.shape
    words = np.ascontiguousarray(words).reshape(g, 128, n, -1)
    if fmt == "e4m3":
        vals = words.view(ml_dtypes.float8_e4m3fn).astype(np.float64)
    else:
        nib = np.empty((g, 128, n, 4), np.uint8)
        nib[..., 0::2] = words & 0xF
        nib[..., 1::2] = words >> 4
        vals = E2M1[nib]
    vals = vals * np.repeat(np.exp2(scales.astype(np.float64) - 127.0), 8, axis=1)[..., None]
    return vals.transpose(0, 1, 3, 2).reshape(g * 512, n)


def gelu(v):
    return 0.5 * v * (1.0 + np.tanh(np.sqrt(2.0 / np.pi) * (v + 0.044715 * v**3)))


K, T, S, T2, P, H, N = 1536, 2048, 512, 1024, 512, 1024, 512


def setup_inputs():
    n = np.random.standard_normal
    s = mx_kscale(K)[:, None]
    u = mx_kscale(H)[:, None]
    tab_words, tab_scales = pack_weight(n((K, T)) * s, "e4m3")
    w4_words, w4_scales = pack_weight(n((H, N)) / np.sqrt(H) / u, "e2m1")
    return {
        "tab_words": tab_words,
        "tab_scales": tab_scales,
        "offs": striped(np.random.permutation(T)[:S]),
        "offs2": striped(np.random.permutation(T2)[:S]),
        "offs3": striped(np.random.permutation(T2)[:P]),
        "offs4": striped(np.random.permutation(T2)[:P]),
        "w1": (n((K, H)) / np.sqrt(K) / s * u.T).astype(np.float32),
        "cap": (0.5 * n(H) * u[:, 0]).astype(np.float32),
        "page0": (n((H, T2)) * u).astype(np.float32),
        "wgs": np.exp(0.3 * n((128, S))).astype(np.float32),
        "gain": (0.6 + 0.3 * n(H)).astype(np.float32),
        "w2": (n((H, N)) / np.sqrt(H) / u).astype(np.float32),
        "w4_words": w4_words,
        "w4_scales": w4_scales,
        "bias": (0.5 * n(N)).astype(np.float32),
    }


def reference(tab_words, tab_scales, offs, offs2, offs3, offs4, w1, cap, page0, wgs, gain, w2, w4_words, w4_scales, bias):
    v = unpack_weight(tab_words, tab_scales, "e4m3")[:, unstriped(offs)]
    h = np.minimum(mxq(f64(w1), 0, "e4m3").T @ v, f64(cap)[:, None])
    before = f64(page0)
    page = before.copy()
    page[:, unstriped(offs2)] = np.tile(f64(wgs), (H // 128, 1)) * h
    earlier = before[:, unstriped(offs4)]
    x = np.maximum(page[:, unstriped(offs3)] - earlier, f64(gain)[:, None] * earlier)
    xq = mxq(x, 0, "e4m3")
    y2 = mxq(f64(w2), 0, "e4m3").T @ xq
    y4 = unpack_weight(w4_words, w4_scales, "e2m1").T @ xq
    return np.minimum(y2, y4) + f64(bias)[:, None]

@@ -1,0 +1,416 @@
+from contextlib import ExitStack
+
+import concourse.mybir as mybir
+from concourse.masks import make_identity
+
+K, T, S, T2, PICK, H, N = 1536, 2048, 512, 1024, 512, 1024, 512
+FLOPS = 2 * K * H * S + 2 * 2 * H * N * PICK
+
+F32 = mybir.dt.float32
+BF16 = mybir.dt.bfloat16
+I32 = mybir.dt.int32
+U32 = mybir.dt.uint32
+U16 = mybir.dt.uint16
+U8 = mybir.dt.uint8
+FP8X4 = mybir.dt.float8_e4m3fn_x4
+FP4X4 = mybir.dt.float4_e2m1fn_x4
+ALU = mybir.AluOpType
+ACT = mybir.ActivationFunctionType
+
+P = 128
+PACK = 4
+K_PASS = P * PACK
+K_PASSES = K // K_PASS
+R_PASSES = H // K_PASS
+QUADS = 4
+N_BLOCKS = N // P
+HALF = PICK // 2
+
+
+def tile_list_mussel_relocation_scores_kernel(
+    tc, tab_words, tab_scales, offs, offs2, offs3, offs4, w1, cap, page0, wgs, gain, w2, w4_words, w4_scales, bias, out
+):
+    nc = tc.nc
+    with ExitStack() as ctx:
+        keep = ctx.enter_context(tc.tile_pool(name="keep", bufs=1))
+        ring = ctx.enter_context(tc.tile_pool(name="ring", bufs=2))
+        psum = ctx.enter_context(tc.psum_pool(name="psum", bufs=1))
+        ctx.enter_context(nc.allow_non_contiguous_dma(reason="per-row vectors, one value a partition"))
+
+        def bank(number, shape, dtype, name):
+            return psum.tile(shape, dtype, name=name, tag=f"bank{number}")
+
+        tab_s = keep.tile([P, T], U8, name="tab_s", align_bytes=64)
+        nc.vector.memset(tab_s[:].bitcast(I32), 0)
+        cap_lo = keep.tile([P, PACK], F32, name="cap_lo")
+        gain_lo = keep.tile([P, PACK], F32, name="gain_lo")
+        nc.gpsimd.dma_start(out=cap_lo[:], in_=cap[0:K_PASS].rearrange("(s p) -> p s", p=P))
+        nc.gpsimd.dma_start(out=gain_lo[:], in_=gain[0:K_PASS].rearrange("(s p) -> p s", p=P))
+        w4_s = keep.tile([P, R_PASSES, N], U8, name="w4_s", align_bytes=64)
+        nc.gpsimd.memset(w4_s[:].rearrange("p a n -> p (a n)").bitcast(I32), 0)
+        ident_bf = keep.tile([P, P], BF16, name="ident_bf")
+        ident_f = keep.tile([P, P], F32, name="ident_f")
+        make_identity(nc, ident_bf[:])
+        make_identity(nc, ident_f[:])
+
+        def load_list(source, name):
+            tile = keep.tile([P, S // 16], U16, name=name)
+            nc.sync.dma_start(tile[:], source)
+            return tile
+
+        def load_table(a):
+            tile = keep.tile([P, T], I32, name=f"tab_w{a}", align_bytes=64)
+            nc.sync.dma_start(out=tile[:], in_=tab_words[a].rearrange("p t i -> p (t i)").bitcast(I32))
+            return tile
+
+        def load_weight(weight, a, c0, c1, name):
+            tile = keep.tile([P, PACK, c1 - c0], F32, name=name)
+            source = weight[a * K_PASS : (a + 1) * K_PASS, c0:c1]
+            nc.sync.dma_start(out=tile[:], in_=source.rearrange("(p j) c -> p j c", j=PACK))
+            return tile
+
+        def load_page(s):
+            tile = keep.tile([P, T2], F32, name=f"page{s}")
+            if s < PACK:
+                source = page0[s * P : (s + 1) * P, :]
+            else:
+                source = page0[K_PASS:H, :].rearrange("(p t) c -> t p c", t=PACK)[s - PACK]
+            nc.sync.dma_start(out=tile[:], in_=source)
+            return tile
+
+        tab_w = [load_table(0)]
+        pick = load_list(offs, "pick")
+        tab_w.append(load_table(1))
+        rows = PACK * K_PASSES
+        for q in range(QUADS):
+            nc.sync.dma_start(
+                out=tab_s[32 * q : 32 * q + rows, :].bitcast(I32),
+                in_=tab_scales[:, PACK * q : PACK * (q + 1), :].bitcast(I32),
+            )
+        tab_w.append(load_table(2))
+        old = load_list(offs4, "old")
+        page = []
+        w1_lo = {}
+        for s in range(PACK):
+            raw = keep.tile([P, K_PASSES, PACK, P], F32, name=f"w1_lo{s}", tag=f"lo_raw{s}", align_bytes=64)
+            for a in range(K_PASSES):
+                source = w1[a * K_PASS : (a + 1) * K_PASS, s * P : (s + 1) * P]
+                nc.sync.dma_start(out=raw[:, a], in_=source.rearrange("(p j) c -> p j c", j=PACK))
+            w1_lo[s] = raw
+            page.append(load_page(s))
+            if s == 0:
+                put = load_list(offs2, "put")
+                wgs_lo = keep.tile([P, S], F32, name="wgs_lo")
+                nc.sync.dma_start(out=wgs_lo[:], in_=wgs)
+                new = load_list(offs3, "new")
+        w1_hi = [load_weight(w1, a, K_PASS, H, f"w1_hi{a}") for a in range(K_PASSES)]
+        w2_raw = [load_weight(w2, a, 0, N, f"w2_raw{a}") for a in range(R_PASSES)]
+        cap_hi = keep.tile([P, PACK], F32, name="cap_hi")
+        gain_hi = keep.tile([P, PACK], F32, name="gain_hi")
+        nc.sync.dma_start(out=cap_hi[:], in_=cap[K_PASS:H].rearrange("(p t) -> p t", t=PACK))
+        nc.sync.dma_start(out=gain_hi[:], in_=gain[K_PASS:H].rearrange("(p t) -> p t", t=PACK))
+        page.append(load_page(PACK))
+        wgs_hi = keep.tile([P, PACK, S], F32, name="wgs_hi")
+        for q in range(QUADS):
+            nc.sync.dma_start(
+                out=wgs_hi[32 * q : 32 * (q + 1)].rearrange("p t j -> p (t j)"),
+                in_=wgs.rearrange("(p t) j -> p (t j)", t=PACK),
+            )
+        for s in range(PACK + 1, 2 * PACK):
+            page.append(load_page(s))
+        w4_w = keep.tile([P, R_PASSES, 2 * N], U8, name="w4_w", align_bytes=64)
+        nc.sync.dma_start(out=w4_w[:].bitcast(I32), in_=w4_words.rearrange("a p c -> p a c").bitcast(I32))
+        for q in range(QUADS):
+            nc.sync.dma_start(
+                out=w4_s[32 * q : 32 * q + PACK].bitcast(I32),
+                in_=w4_scales[:, PACK * q : PACK * (q + 1), :].rearrange("a r n -> r a n").bitcast(I32),
+            )
+        bias_c = keep.tile([P, N_BLOCKS], F32, name="bias_c")
+        nc.sync.dma_start(out=bias_c[:], in_=bias.rearrange("(b p) -> p b", p=P))
+
+        v_s = keep.tile([P, S], U8, name="v_s", align_bytes=64)
+        v_w = []
+        for a in range(K_PASSES):
+            words = keep.tile([P, S], U32, name=f"v_w{a}", align_bytes=64)
+            nc.vector.tensor_copy(words[:], tab_w[a][:].bitcast(U32).indirect(pick[:]))
+            v_w.append(words)
+            if a == 1:
+                nc.vector.tensor_copy(v_s[:], tab_s[:].indirect(pick[:]))
+
+        def interleave(grouped, raw):
+            nc.scalar.copy(
+                out=grouped.rearrange("p (c i j) -> p c j i", i=PACK, j=PACK),
+                in_=raw.rearrange("p j (c i) -> p c j i", i=PACK),
+            )
+
+        def quantize(codes, scales, grouped):
+            nc.vector.quantize_mx(out=codes.bitcast(FP8X4), scales=scales, in_=grouped)
+
+        w1_c = {}
+        w1_s = {}
+
+        w1_g = {}
+
+        def round_w1(s):
+            if s < 2 * PACK - 2:
+                grouped = ring.tile([P, K_PASSES, P * PACK], BF16, name="w1_grouped", align_bytes=64)[:]
+            else:
+                if s == 2 * PACK - 2:
+                    w1_g["late"] = keep.tile(
+                        [P, 2, K_PASSES, P * PACK], BF16, name="w1_late", tag="lo_raw0", align_bytes=64
+                    )
+                grouped = w1_g["late"][:, s - (2 * PACK - 2)]
+            for a in range(K_PASSES):
+                if s < PACK:
+                    interleave(grouped[:, a, :], w1_lo[s][:, a])
+                else:
+                    nc.scalar.copy(
+                        out=grouped[:, a, :].rearrange("p (m j) -> p m j", j=PACK),
+                        in_=w1_hi[a][:].rearrange("p j (m t) -> p t m j", t=PACK)[:, s - PACK],
+                    )
+            w1_g[s] = grouped
+
+        def quantize_w1(s):
+            grouped = w1_g[s]
+            codes = keep.tile([P, K_PASSES, P], U32, name=f"w1_c{s}", tag=f"w1_c{s}", align_bytes=64)
+            scales = keep.tile([P, K_PASSES, P], U8, name=f"w1_s{s}", align_bytes=64)
+            for a in range(K_PASSES):
+                if s == 0:
+                    quantize(codes[:, a, :], scales[:, a, :], grouped[:, a, :])
+                w1_c[s, a] = codes[:, a, :]
+                w1_s[s, a] = scales[:, a, :]
+            if s > 0:
+                quantize(
+                    codes[:].rearrange("p a c -> p (a c)"),
+                    scales[:].rearrange("p a c -> p (a c)"),
+                    grouped.rearrange("p a c -> p (a c)"),
+                )
+
+        h_banks = [0, 1, 2, 3]
+        sums = {}
+
+        def first_product(s):
+            acc = bank(h_banks[s % 4], [P, S], F32, f"h_sum{s}")
+            for a in range(K_PASSES):
+                nc.tensor.matmul_mx(
+                    out=acc[:],
+                    lhsT=w1_c[s, a].bitcast(FP8X4),
+                    lhsT_scale=w1_s[s, a],
+                    rhs=v_w[a][:].bitcast(FP8X4),
+                    rhs_scale=v_s[PACK * a : P, :],
+                    start=(a == 0),
+                    stop=(a == K_PASSES - 1),
+                )
+            sums[s] = acc
+
+        capped = {}
+
+        def cap_rows(s):
+            h = ring.tile([P, S], F32, name="h")
+            limit = cap_lo[:, s : s + 1] if s < PACK else cap_hi[:, s - PACK : s - PACK + 1]
+            nc.vector.tensor_scalar(out=h[:], in0=sums[s][:], scalar1=limit, scalar2=None, op0=ALU.min)
+            capped[s] = h
+
+        ge_hi = keep.tile([P, PACK, PICK], F32, name="ge_hi")
+        d_hi = keep.tile([P, PACK, PICK], F32, name="d_hi")
+        e_first = keep.tile([P, PICK], F32, name="e_first")
+        e_hi = keep.tile([P, PACK, PICK], F32, name="e_hi")
+        d_last_lo = keep.tile([P, PICK], F32, name="d_last_lo")
+        picked = {}
+
+        def earlier(s):
+            if s == 0:
+                return e_first[:]
+            if s >= PACK:
+                return e_hi[:, s - PACK, :]
+            if s not in picked:
+                picked[s] = keep.tile([P, 2, PICK], F32, name=f"picked{s}", tag=f"lo_raw{s}", align_bytes=64)
+            return picked[s][:, 0, :]
+
+        def fetch_old(s):
+            nc.vector.tensor_copy(earlier(s), page[s][:].indirect(old[:]))
+
+        def scale_old(t):
+            nc.scalar.activation(out=ge_hi[:, t, :], in_=e_hi[:, t, :], func=ACT.Copy, scale=gain_hi[:, t : t + 1])
+
+        def put_new(s):
+            weights = wgs_lo[:] if s < PACK else wgs_hi[:, s - PACK, :]
+            nc.vector.tensor_tensor(page[s][:].indirect(put[:]), capped[s][:], weights, ALU.mult)
+
+        def fetch_new(s, d, m0, m1):
+            nc.vector.tensor_tensor(
+                d, page[s][:].indirect(new[:, m0 // 16 : m1 // 16]), earlier(s)[:, m0:m1], ALU.subtract
+            )
+
+        x_t = keep.tile([P, PICK // P, K_PASS], BF16, name="x_t")
+        d_lo = {}
+
+        def diff_lo(s):
+            d_lo[s] = picked[s + 1][:, 1, :] if s + 1 < PACK else d_last_lo[:]
+            fetch_new(s, d_lo[s], 0, PICK)
+
+        x_lo = {}
+
+        def finish_lo(s):
+            x = keep.tile([P, PICK], BF16, name=f"x_lo{s}", tag=f"w1_c{s + 1}", align_bytes=64)
+            nc.vector.scalar_tensor_tensor(
+                out=x[:], in0=earlier(s), scalar=gain_lo[:, s : s + 1], in1=d_lo[s], op0=ALU.mult, op1=ALU.max
+            )
+            x_lo[s] = x
+
+        def turn_lo(pair):
+            turned = bank(pair, [P, 2, PICK // P, P], BF16, f"turned{pair}")
+            for i in range(2):
+                for mb in range(PICK // P):
+                    nc.tensor.transpose(turned[:, i, mb, :], x_lo[2 * pair + i][:, mb * P : (mb + 1) * P], ident_bf[:])
+            nc.scalar.copy(
+                out=x_t[:, :, 2 * pair * P : 2 * (pair + 1) * P].rearrange("p b (i r) -> p i b r", i=2), in_=turned[:]
+            )
+
+        x_g = [keep.tile([P, PICK, PACK], BF16, name=f"x_g{b}", align_bytes=64) for b in range(R_PASSES)]
+        x_c = [keep.tile([P, PICK], U32, name=f"x_c{b}", align_bytes=64) for b in range(R_PASSES)]
+        x_s = [keep.tile([P, PICK], U8, name=f"x_s{b}", align_bytes=64) for b in range(R_PASSES)]
+
+        def regroup_lo():
+            target = x_g[0][:].rearrange("p m t -> p (m t)").bitcast(F32)
+            for pair in range(2):
+                back = bank(4 + pair, [P, 2, 2, P], F32, f"back{pair}")
+                for i in range(2):
+                    words = x_t[:, 2 * pair + i, :].bitcast(F32)
+                    for u in range(2):
+                        nc.tensor.transpose(back[:, i, u, :], words[:, u : 2 * P : 2], ident_f[:])
+                nc.scalar.copy(
+                    out=target[:, pair * 4 * P : (pair + 1) * 4 * P].rearrange("p (i m u) -> p i m u", i=2, u=2),
+                    in_=back[:].rearrange("p i u m -> p i m u"),
+                )
+
+        def quantize_x(b, m0, m1):
+            quantize(x_c[b][:, m0:m1], x_s[b][:, m0:m1], x_g[b][:, m0:m1, :].rearrange("p m t -> p (m t)"))
+
+        def finish_hi(m0, m1):
+            nc.vector.tensor_tensor(
+                x_g[1][:, m0:m1, :].rearrange("p (c i) t -> p c t i", i=2),
+                d_hi[:, :, m0:m1].rearrange("p t (c i) -> p c t i", i=2),
+                ge_hi[:, :, m0:m1].rearrange("p t (c i) -> p c t i", i=2),
+                ALU.max,
+            )
+
+        w2_c = []
+        w2_s = []
+
+        w2_g = []
+
+        def round_w2(a):
+            grouped = ring.tile([P, N * PACK], BF16, name="w2_grouped", align_bytes=64)
+            interleave(grouped[:], w2_raw[a][:])
+            w2_g.append(grouped)
+
+        def quantize_w2(a):
+            codes = keep.tile([P, N], U32, name=f"w2_c{a}", align_bytes=64)
+            scales = keep.tile([P, N], U8, name=f"w2_s{a}", align_bytes=64)
+            quantize(codes[:], scales[:], w2_g[a][:])
+            w2_c.append(codes)
+            w2_s.append(scales)
+
+        y_banks = {}
+
+        def open_scores(half):
+            for kind in range(2):
+                for pair in range(2):
+                    number = [[6, 4], [0, 2]][half][kind] + pair
+                    y_banks[half, kind, pair] = bank(number, [P, 2, HALF], F32, f"y{half}{kind}{pair}")
+
+        def second_pass(half, b):
+            cols = slice(half * HALF, (half + 1) * HALF)
+            for pair in range(2):
+                for kind in range(2):
+                    for i in range(2):
+                        nb = 2 * pair + i
+                        if kind == 0:
+                            codes = w4_w[:, b, 2 * P * nb : 2 * P * (nb + 1)].bitcast(FP4X4)
+                            scales = w4_s[:, b, P * nb : P * (nb + 1)]
+                        else:
+                            codes = w2_c[b][:, P * nb : P * (nb + 1)].bitcast(FP8X4)
+                            scales = w2_s[b][:, P * nb : P * (nb + 1)]
+                        nc.tensor.matmul_mx(
+                            out=y_banks[half, kind, pair][:, i, :],
+                            lhsT=codes,
+                            lhsT_scale=scales,
+                            rhs=x_c[b][:, cols].bitcast(FP8X4),
+                            rhs_scale=x_s[b][:, cols],
+                            start=(b == 0 and i == 0),
+                            stop=(b == R_PASSES - 1 and i == 1),
+                        )
+
+        def scores_out(half):
+            for pair in range(2):
+                y4 = ring.tile([P, 2, HALF], F32, name="y4")
+                result = ring.tile([P, 2, HALF], F32, name="result", bufs=4)
+                for i in range(2):
+                    nb = 2 * pair + i
+                    nc.scalar.activation(
+                        out=y4[:, i, :],
+                        in_=y_banks[half, 0, pair][:, i, :],
+                        func=ACT.Identity,
+                        bias=bias_c[:, nb : nb + 1],
+                    )
+                    nc.vector.scalar_tensor_tensor(
+                        out=result[:, i, :],
+                        in0=y_banks[half, 1, pair][:, i, :],
+                        scalar=bias_c[:, nb : nb + 1],
+                        in1=y4[:, i, :],
+                        op0=ALU.add,
+                        op1=ALU.min,
+                    )
+                target = out[pair * 2 * P : (pair + 1) * 2 * P, half * HALF : (half + 1) * HALF]
+                nc.sync.dma_start(out=target.rearrange("(i p) m -> p i m", p=P), in_=result[:])
+
+        last = 2 * PACK - 1
+        round_w1(0)
+        quantize_w1(0)
+        first_product(0)
+        fetch_old(0)
+        cap_rows(0)
+        for s in range(2 * PACK):
+            put_new(s)
+            if s < PACK:
+                round_w1(s + 1)
+            if s < last:
+                quantize_w1(s + 1)
+                first_product(s + 1)
+            if s == PACK - 1:
+                for later in range(PACK + 1, 2 * PACK):
+                    round_w1(later)
+                for a in range(R_PASSES):
+                    round_w2(a)
+            if s < last:
+                fetch_old(s + 1)
+            if s < PACK:
+                diff_lo(s)
+            elif s < last:
+                fetch_new(s, d_hi[:, s - PACK, :], 0, PICK)
+            if s < last:
+                cap_rows(s + 1)
+            if s < PACK:
+                finish_lo(s)
+            if s == PACK:
+                for pair in range(2):
+                    turn_lo(pair)
+                regroup_lo()
+            if s == last - 1:
+                for a in range(R_PASSES):
+                    quantize_w2(a)
+                quantize_x(0, 0, PICK)
+                for half in range(2):
+                    open_scores(half)
+                    second_pass(half, 0)
+        for t in range(PACK):
+            scale_old(t)
+        for half in range(2):
+            fetch_new(last, d_hi[:, PACK - 1, half * HALF : (half + 1) * HALF], half * HALF, (half + 1) * HALF)
+        for half in range(2):
+            finish_hi(half * HALF, (half + 1) * HALF)
+            quantize_x(1, half * HALF, (half + 1) * HALF)
+            second_pass(half, 1)
+        for half in range(2):
+            scores_out(half)

@@ -31,6 +31,7 @@ def tile_list_mussel_relocation_scores_kernel(
     tc, tab_words, tab_scales, offs, offs2, offs3, offs4, w1, cap, page0, wgs, gain, w2, w4_words, w4_scales, bias, out
 ):
     nc = tc.nc
+    last = 2 * PACK - 1
     with ExitStack() as ctx:
         keep = ctx.enter_context(tc.tile_pool(name="keep", bufs=1))
         ring = ctx.enter_context(tc.tile_pool(name="ring", bufs=2))
@@ -78,6 +79,16 @@ def tile_list_mussel_relocation_scores_kernel(
             nc.sync.dma_start(out=tile[:], in_=source)
             return tile
 
+        w1_lo = {}
+
+        def load_w1_lo(s):
+            raw = keep.tile([P, K_PASSES, PACK, P], F32, name=f"w1_lo{s}", tag=f"lo_raw{s}", align_bytes=64)
+            for a in range(K_PASSES):
+                source = w1[a * K_PASS : (a + 1) * K_PASS, s * P : (s + 1) * P]
+                nc.sync.dma_start(out=raw[:, a], in_=source.rearrange("(p j) c -> p j c", j=PACK))
+            w1_lo[s] = raw
+
+        load_w1_lo(0)
         tab_w = [load_table(0)]
         pick = load_list(offs, "pick")
         tab_w.append(load_table(1))
@@ -88,21 +99,15 @@ def tile_list_mussel_relocation_scores_kernel(
                 in_=tab_scales[:, PACK * q : PACK * (q + 1), :].bitcast(I32),
             )
         tab_w.append(load_table(2))
+        page = [load_page(0)]
         old = load_list(offs4, "old")
-        page = []
-        w1_lo = {}
-        for s in range(PACK):
-            raw = keep.tile([P, K_PASSES, PACK, P], F32, name=f"w1_lo{s}", tag=f"lo_raw{s}", align_bytes=64)
-            for a in range(K_PASSES):
-                source = w1[a * K_PASS : (a + 1) * K_PASS, s * P : (s + 1) * P]
-                nc.sync.dma_start(out=raw[:, a], in_=source.rearrange("(p j) c -> p j c", j=PACK))
-            w1_lo[s] = raw
+        put = load_list(offs2, "put")
+        wgs_lo = keep.tile([P, S], F32, name="wgs_lo")
+        nc.sync.dma_start(out=wgs_lo[:], in_=wgs)
+        new = load_list(offs3, "new")
+        for s in range(1, PACK):
+            load_w1_lo(s)
             page.append(load_page(s))
-            if s == 0:
-                put = load_list(offs2, "put")
-                wgs_lo = keep.tile([P, S], F32, name="wgs_lo")
-                nc.sync.dma_start(out=wgs_lo[:], in_=wgs)
-                new = load_list(offs3, "new")
         w1_hi = [load_weight(w1, a, K_PASS, H, f"w1_hi{a}") for a in range(K_PASSES)]
         w2_raw = [load_weight(w2, a, 0, N, f"w2_raw{a}") for a in range(R_PASSES)]
         cap_hi = keep.tile([P, PACK], F32, name="cap_hi")
@@ -111,7 +116,7 @@ def tile_list_mussel_relocation_scores_kernel(
         nc.sync.dma_start(out=gain_hi[:], in_=gain[K_PASS:H].rearrange("(p t) -> p t", t=PACK))
         page.append(load_page(PACK))
         wgs_hi = keep.tile([P, PACK, S], F32, name="wgs_hi")
-        for q in range(QUADS):
+        for q in (0, 2, 1, 3):
             nc.sync.dma_start(
                 out=wgs_hi[32 * q : 32 * (q + 1)].rearrange("p t j -> p (t j)"),
                 in_=wgs.rearrange("(p t) j -> p (t j)", t=PACK),
@@ -151,15 +156,18 @@ def tile_list_mussel_relocation_scores_kernel(
 
         w1_g = {}
 
+        def stage_tag(s):
+            if s <= PACK:
+                return f"lo_raw{s % PACK}"
+            return f"hi_grouped{s}"
+
         def round_w1(s):
-            if s < 2 * PACK - 2:
+            if s < PACK:
                 grouped = ring.tile([P, K_PASSES, P * PACK], BF16, name="w1_grouped", align_bytes=64)[:]
             else:
-                if s == 2 * PACK - 2:
-                    w1_g["late"] = keep.tile(
-                        [P, 2, K_PASSES, P * PACK], BF16, name="w1_late", tag="lo_raw0", align_bytes=64
-                    )
-                grouped = w1_g["late"][:, s - (2 * PACK - 2)]
+                grouped = keep.tile(
+                    [P, K_PASSES, P * PACK], BF16, name=f"w1_grouped{s}", tag=stage_tag(s), align_bytes=64
+                )[:]
             for a in range(K_PASSES):
                 if s < PACK:
                     interleave(grouped[:, a, :], w1_lo[s][:, a])
@@ -206,57 +214,51 @@ def tile_list_mussel_relocation_scores_kernel(
         capped = {}
 
         def cap_rows(s):
-            h = ring.tile([P, S], F32, name="h")
+            h = keep.tile([P, S], F32, name=f"h{s}", tag=f"h{s % 2}", align_bytes=64)
             limit = cap_lo[:, s : s + 1] if s < PACK else cap_hi[:, s - PACK : s - PACK + 1]
             nc.vector.tensor_scalar(out=h[:], in0=sums[s][:], scalar1=limit, scalar2=None, op0=ALU.min)
             capped[s] = h
 
-        ge_hi = keep.tile([P, PACK, PICK], F32, name="ge_hi")
-        d_hi = keep.tile([P, PACK, PICK], F32, name="d_hi")
         e_first = keep.tile([P, PICK], F32, name="e_first")
-        e_hi = keep.tile([P, PACK, PICK], F32, name="e_hi")
-        d_last_lo = keep.tile([P, PICK], F32, name="d_last_lo")
+        d_last = keep.tile([P, PICK], F32, name="d_last")
         picked = {}
 
         def earlier(s):
-            if s == 0:
-                return e_first[:]
-            if s >= PACK:
-                return e_hi[:, s - PACK, :]
-            if s not in picked:
-                picked[s] = keep.tile([P, 2, PICK], F32, name=f"picked{s}", tag=f"lo_raw{s}", align_bytes=64)
-            return picked[s][:, 0, :]
+            return e_first[:] if s == 0 else picked[s][:, 0, :]
+
+        def change(s):
+            return d_last[:] if s == last else picked[s + 1][:, 1, :]
 
         def fetch_old(s):
             nc.vector.tensor_copy(earlier(s), page[s][:].indirect(old[:]))
-
-        def scale_old(t):
-            nc.scalar.activation(out=ge_hi[:, t, :], in_=e_hi[:, t, :], func=ACT.Copy, scale=gain_hi[:, t : t + 1])
 
         def put_new(s):
             weights = wgs_lo[:] if s < PACK else wgs_hi[:, s - PACK, :]
             nc.vector.tensor_tensor(page[s][:].indirect(put[:]), capped[s][:], weights, ALU.mult)
 
-        def fetch_new(s, d, m0, m1):
+        def fetch_new(s, m0, m1):
             nc.vector.tensor_tensor(
-                d, page[s][:].indirect(new[:, m0 // 16 : m1 // 16]), earlier(s)[:, m0:m1], ALU.subtract
+                change(s)[:, m0:m1], page[s][:].indirect(new[:, m0 // 16 : m1 // 16]), earlier(s)[:, m0:m1], ALU.subtract
             )
 
         x_t = keep.tile([P, PICK // P, K_PASS], BF16, name="x_t")
-        d_lo = {}
-
-        def diff_lo(s):
-            d_lo[s] = picked[s + 1][:, 1, :] if s + 1 < PACK else d_last_lo[:]
-            fetch_new(s, d_lo[s], 0, PICK)
-
+        x_hi = keep.tile([P, PACK, PICK], BF16, name="x_hi")
         x_lo = {}
 
-        def finish_lo(s):
-            x = keep.tile([P, PICK], BF16, name=f"x_lo{s}", tag=f"w1_c{s + 1}", align_bytes=64)
+        def finish(s, m0, m1):
+            if s < PACK:
+                x_lo[s] = keep.tile([P, PICK], BF16, name=f"x_lo{s}", tag=f"w1_c{s + 1}", align_bytes=64)
+                x, factor = x_lo[s][:], gain_lo[:, s : s + 1]
+            else:
+                x, factor = x_hi[:, s - PACK, :], gain_hi[:, s - PACK : s - PACK + 1]
             nc.vector.scalar_tensor_tensor(
-                out=x[:], in0=earlier(s), scalar=gain_lo[:, s : s + 1], in1=d_lo[s], op0=ALU.mult, op1=ALU.max
+                out=x[:, m0:m1],
+                in0=earlier(s)[:, m0:m1],
+                scalar=factor,
+                in1=change(s)[:, m0:m1],
+                op0=ALU.mult,
+                op1=ALU.max,
             )
-            x_lo[s] = x
 
         def turn_lo(pair):
             turned = bank(pair, [P, 2, PICK // P, P], BF16, f"turned{pair}")
@@ -268,7 +270,7 @@ def tile_list_mussel_relocation_scores_kernel(
             )
 
         x_g = [keep.tile([P, PICK, PACK], BF16, name=f"x_g{b}", align_bytes=64) for b in range(R_PASSES)]
-        x_c = [keep.tile([P, PICK], U32, name=f"x_c{b}", align_bytes=64) for b in range(R_PASSES)]
+        x_c = {}
         x_s = [keep.tile([P, PICK], U8, name=f"x_s{b}", align_bytes=64) for b in range(R_PASSES)]
 
         def regroup_lo():
@@ -285,14 +287,14 @@ def tile_list_mussel_relocation_scores_kernel(
                 )
 
         def quantize_x(b, m0, m1):
+            if b not in x_c:
+                x_c[b] = keep.tile([P, PICK], U32, name=f"x_c{b}", tag=f"h{1 - b}", align_bytes=64)
             quantize(x_c[b][:, m0:m1], x_s[b][:, m0:m1], x_g[b][:, m0:m1, :].rearrange("p m t -> p (m t)"))
 
-        def finish_hi(m0, m1):
-            nc.vector.tensor_tensor(
-                x_g[1][:, m0:m1, :].rearrange("p (c i) t -> p c t i", i=2),
-                d_hi[:, :, m0:m1].rearrange("p t (c i) -> p c t i", i=2),
-                ge_hi[:, :, m0:m1].rearrange("p t (c i) -> p c t i", i=2),
-                ALU.max,
+        def regroup_hi(copy, m0, m1):
+            copy(
+                x_g[1][:, m0:m1, :].rearrange("p (c i) t -> p c t i", i=PACK),
+                x_hi[:, :, m0:m1].rearrange("p t (c i) -> p c t i", i=PACK),
             )
 
         w2_c = []
@@ -365,7 +367,6 @@ def tile_list_mussel_relocation_scores_kernel(
                 target = out[pair * 2 * P : (pair + 1) * 2 * P, half * HALF : (half + 1) * HALF]
                 nc.sync.dma_start(out=target.rearrange("(i p) m -> p i m", p=P), in_=result[:])
 
-        last = 2 * PACK - 1
         round_w1(0)
         quantize_w1(0)
         first_product(0)
@@ -383,16 +384,19 @@ def tile_list_mussel_relocation_scores_kernel(
                     round_w1(later)
                 for a in range(R_PASSES):
                     round_w2(a)
-            if s < last:
+            if s == last:
+                break
+            picked[s + 1] = keep.tile([P, 2, PICK], F32, name=f"picked{s + 1}", tag=stage_tag(s + 1), align_bytes=64)
+            if s < PACK:
                 fetch_old(s + 1)
-            if s < PACK:
-                diff_lo(s)
-            elif s < last:
-                fetch_new(s, d_hi[:, s - PACK, :], 0, PICK)
-            if s < last:
+                fetch_new(s, 0, PICK)
                 cap_rows(s + 1)
-            if s < PACK:
-                finish_lo(s)
+                finish(s, 0, PICK)
+            else:
+                fetch_new(s, 0, PICK)
+                fetch_old(s + 1)
+                finish(s, 0, PICK)
+                cap_rows(s + 1)
             if s == PACK:
                 for pair in range(2):
                     turn_lo(pair)
@@ -400,16 +404,17 @@ def tile_list_mussel_relocation_scores_kernel(
             if s == last - 1:
                 for a in range(R_PASSES):
                     quantize_w2(a)
-                quantize_x(0, 0, PICK)
-                for half in range(2):
-                    open_scores(half)
-                    second_pass(half, 0)
-        for t in range(PACK):
-            scale_old(t)
+        quantize_x(0, 0, PICK)
         for half in range(2):
-            fetch_new(last, d_hi[:, PACK - 1, half * HALF : (half + 1) * HALF], half * HALF, (half + 1) * HALF)
+            open_scores(half)
+            second_pass(half, 0)
+        fetch_new(last, 0, HALF)
+        fetch_new(last, HALF, PICK)
+        finish(last, 0, HALF)
+        regroup_hi(nc.scalar.copy, 0, HALF)
+        finish(last, HALF, PICK)
+        regroup_hi(nc.vector.tensor_copy, HALF, PICK)
         for half in range(2):
-            finish_hi(half * HALF, (half + 1) * HALF)
             quantize_x(1, half * HALF, (half + 1) * HALF)
             second_pass(half, 1)
         for half in range(2):

@@ -180,7 +180,8 @@ def tile_list_mussel_relocation_scores_kernel(
 
         def quantize_w1(s):
             grouped = w1_g[s]
-            codes = keep.tile([P, K_PASSES, P], U32, name=f"w1_c{s}", tag=f"w1_c{s}", align_bytes=64)
+            tag = f"w1_c{s}" if s <= PACK else stage_tag(s - 2)
+            codes = keep.tile([P, K_PASSES, P], U32, name=f"w1_c{s}", tag=tag, align_bytes=64)
             scales = keep.tile([P, K_PASSES, P], U8, name=f"w1_s{s}", align_bytes=64)
             for a in range(K_PASSES):
                 if s == 0:
@@ -308,7 +309,7 @@ def tile_list_mussel_relocation_scores_kernel(
             w2_g.append(grouped)
 
         def quantize_w2(a):
-            codes = keep.tile([P, N], U32, name=f"w2_c{a}", align_bytes=64)
+            codes = keep.tile([P, N], U32, name=f"w2_c{a}", tag=stage_tag(PACK + a), align_bytes=64)
             scales = keep.tile([P, N], U8, name=f"w2_s{a}", align_bytes=64)
             quantize(codes[:], scales[:], w2_g[a][:])
             w2_c.append(codes)

@@ -108,20 +108,22 @@ def tile_list_mussel_relocation_scores_kernel(
         for s in range(1, PACK):
             load_w1_lo(s)
             page.append(load_page(s))
-        w1_hi = [load_weight(w1, a, K_PASS, H, f"w1_hi{a}") for a in range(K_PASSES)]
-        w2_raw = [load_weight(w2, a, 0, N, f"w2_raw{a}") for a in range(R_PASSES)]
+        w1_hi = [load_weight(w1, a, K_PASS, H, f"w1_hi{a}") for a in range(K_PASSES - 1)]
+        page.append(load_page(PACK))
+        w1_hi.append(load_weight(w1, K_PASSES - 1, K_PASS, H, "w1_hi2"))
         cap_hi = keep.tile([P, PACK], F32, name="cap_hi")
         gain_hi = keep.tile([P, PACK], F32, name="gain_hi")
         nc.sync.dma_start(out=cap_hi[:], in_=cap[K_PASS:H].rearrange("(p t) -> p t", t=PACK))
         nc.sync.dma_start(out=gain_hi[:], in_=gain[K_PASS:H].rearrange("(p t) -> p t", t=PACK))
-        page.append(load_page(PACK))
+        w2_raw = [load_weight(w2, a, 0, N, f"w2_raw{a}") for a in range(R_PASSES)]
+        page.append(load_page(PACK + 1))
         wgs_hi = keep.tile([P, PACK, S], F32, name="wgs_hi")
         for q in (0, 2, 1, 3):
             nc.sync.dma_start(
                 out=wgs_hi[32 * q : 32 * (q + 1)].rearrange("p t j -> p (t j)"),
                 in_=wgs.rearrange("(p t) j -> p (t j)", t=PACK),
             )
-        for s in range(PACK + 1, 2 * PACK):
+        for s in range(PACK + 2, 2 * PACK):
             page.append(load_page(s))
         w4_w = keep.tile([P, R_PASSES, 2 * N], U8, name="w4_w", align_bytes=64)
         nc.sync.dma_start(out=w4_w[:].bitcast(I32), in_=w4_words.rearrange("a p c -> p a c").bitcast(I32))
@@ -155,6 +157,7 @@ def tile_list_mussel_relocation_scores_kernel(
         w1_s = {}
 
         w1_g = {}
+        h_tags = ["h_a", "h_b", "h_a", "h_b", "h_a", "h_b", "h_c", "h_a"]
 
         def stage_tag(s):
             if s <= PACK:
@@ -180,15 +183,15 @@ def tile_list_mussel_relocation_scores_kernel(
 
         def quantize_w1(s):
             grouped = w1_g[s]
-            tag = f"w1_c{s}" if s <= PACK else stage_tag(s - 2)
+            tag = f"w1_c{s}" if s < last - 1 else h_tags[s - 2]
             codes = keep.tile([P, K_PASSES, P], U32, name=f"w1_c{s}", tag=tag, align_bytes=64)
             scales = keep.tile([P, K_PASSES, P], U8, name=f"w1_s{s}", align_bytes=64)
             for a in range(K_PASSES):
-                if s == 0:
+                if s <= PACK:
                     quantize(codes[:, a, :], scales[:, a, :], grouped[:, a, :])
                 w1_c[s, a] = codes[:, a, :]
                 w1_s[s, a] = scales[:, a, :]
-            if s > 0:
+            if s > PACK:
                 quantize(
                     codes[:].rearrange("p a c -> p (a c)"),
                     scales[:].rearrange("p a c -> p (a c)"),
@@ -215,27 +218,41 @@ def tile_list_mussel_relocation_scores_kernel(
         capped = {}
 
         def cap_rows(s):
-            h = keep.tile([P, S], F32, name=f"h{s}", tag=f"h{s % 2}", align_bytes=64)
+            h = keep.tile([P, S], F32, name=f"h{s}", tag=h_tags[s], align_bytes=64)
             limit = cap_lo[:, s : s + 1] if s < PACK else cap_hi[:, s - PACK : s - PACK + 1]
-            nc.vector.tensor_scalar(out=h[:], in0=sums[s][:], scalar1=limit, scalar2=None, op0=ALU.min)
+            weights = wgs_lo[:] if s < PACK else wgs_hi[:, s - PACK, :]
+            nc.vector.scalar_tensor_tensor(
+                out=h[:], in0=sums[s][:], scalar=limit, in1=weights, op0=ALU.min, op1=ALU.mult
+            )
             capped[s] = h
 
-        e_first = keep.tile([P, PICK], F32, name="e_first")
-        d_last = keep.tile([P, PICK], F32, name="d_last")
-        picked = {}
+        olds = {}
+        changes = {}
+        old_tags = {0: "old0", 5: stage_tag(3), 6: stage_tag(4), 7: stage_tag(3)}
+        change_tags = {4: "change4", 5: "change5", 6: stage_tag(5), 7: stage_tag(6)}
+
+        def make_room(s):
+            if 1 <= s <= PACK:
+                pair = keep.tile([P, 2, PICK], F32, name=f"picked{s}", tag=stage_tag(s), align_bytes=64)
+                olds[s] = pair[:, 0, :]
+                changes[s - 1] = pair[:, 1, :]
+            else:
+                olds[s] = keep.tile([P, PICK], F32, name=f"old{s}", tag=old_tags[s], align_bytes=64)[:]
 
         def earlier(s):
-            return e_first[:] if s == 0 else picked[s][:, 0, :]
+            return olds[s]
 
         def change(s):
-            return d_last[:] if s == last else picked[s + 1][:, 1, :]
+            if s not in changes:
+                changes[s] = keep.tile([P, PICK], F32, name=f"change{s}", tag=change_tags[s], align_bytes=64)[:]
+            return changes[s]
 
         def fetch_old(s):
+            make_room(s)
             nc.vector.tensor_copy(earlier(s), page[s][:].indirect(old[:]))
 
         def put_new(s):
-            weights = wgs_lo[:] if s < PACK else wgs_hi[:, s - PACK, :]
-            nc.vector.tensor_tensor(page[s][:].indirect(put[:]), capped[s][:], weights, ALU.mult)
+            nc.vector.tensor_copy(page[s][:].indirect(put[:]), capped[s][:])
 
         def fetch_new(s, m0, m1):
             nc.vector.tensor_tensor(
@@ -289,7 +306,7 @@ def tile_list_mussel_relocation_scores_kernel(
 
         def quantize_x(b, m0, m1):
             if b not in x_c:
-                x_c[b] = keep.tile([P, PICK], U32, name=f"x_c{b}", tag=f"h{1 - b}", align_bytes=64)
+                x_c[b] = keep.tile([P, PICK], U32, name=f"x_c{b}", tag=[change_tags[last - 1], "h_c"][b], align_bytes=64)
             quantize(x_c[b][:, m0:m1], x_s[b][:, m0:m1], x_g[b][:, m0:m1, :].rearrange("p m t -> p (m t)"))
 
         def regroup_hi(copy, m0, m1):
@@ -309,7 +326,7 @@ def tile_list_mussel_relocation_scores_kernel(
             w2_g.append(grouped)
 
         def quantize_w2(a):
-            codes = keep.tile([P, N], U32, name=f"w2_c{a}", tag=stage_tag(PACK + a), align_bytes=64)
+            codes = keep.tile([P, N], U32, name=f"w2_c{a}", tag=change_tags[PACK + a], align_bytes=64)
             scales = keep.tile([P, N], U8, name=f"w2_s{a}", align_bytes=64)
             quantize(codes[:], scales[:], w2_g[a][:])
             w2_c.append(codes)
@@ -373,38 +390,38 @@ def tile_list_mussel_relocation_scores_kernel(
         first_product(0)
         fetch_old(0)
         cap_rows(0)
-        for s in range(2 * PACK):
+        for s in range(PACK):
             put_new(s)
-            if s < PACK:
-                round_w1(s + 1)
-            if s < last:
-                quantize_w1(s + 1)
-                first_product(s + 1)
-            if s == PACK - 1:
-                for later in range(PACK + 1, 2 * PACK):
-                    round_w1(later)
-                for a in range(R_PASSES):
-                    round_w2(a)
-            if s == last:
-                break
-            picked[s + 1] = keep.tile([P, 2, PICK], F32, name=f"picked{s + 1}", tag=stage_tag(s + 1), align_bytes=64)
-            if s < PACK:
-                fetch_old(s + 1)
-                fetch_new(s, 0, PICK)
+            round_w1(s + 1)
+            quantize_w1(s + 1)
+            first_product(s + 1)
+            fetch_old(s + 1)
+            fetch_new(s, 0, PICK)
+            cap_rows(s + 1)
+            finish(s, 0, PICK)
+        for s in range(PACK + 1, 2 * PACK):
+            round_w1(s)
+        for a in range(R_PASSES):
+            round_w2(a)
+        quantize_w1(PACK + 1)
+        first_product(PACK + 1)
+        cap_rows(PACK + 1)
+        for pair in range(2):
+            turn_lo(pair)
+        regroup_lo()
+        for s in range(PACK, last):
+            put_new(s)
+            fetch_old(s + 1)
+            fetch_new(s, 0, PICK)
+            if s > PACK:
                 cap_rows(s + 1)
-                finish(s, 0, PICK)
-            else:
-                fetch_new(s, 0, PICK)
-                fetch_old(s + 1)
-                finish(s, 0, PICK)
-                cap_rows(s + 1)
-            if s == PACK:
-                for pair in range(2):
-                    turn_lo(pair)
-                regroup_lo()
-            if s == last - 1:
-                for a in range(R_PASSES):
-                    quantize_w2(a)
+            if s + 2 <= last:
+                quantize_w1(s + 2)
+                first_product(s + 2)
+            finish(s, 0, PICK)
+            if s > PACK:
+                quantize_w2(s - PACK - 1)
+        put_new(last)
         quantize_x(0, 0, PICK)
         for half in range(2):
             open_scores(half)

@@ -23,39 +23,52 @@ K_PASS = P * PACK
 K_PASSES = K // K_PASS
 R_PASSES = H // K_PASS
 QUADS = 4
-N_BLOCKS = N // P
+QUAD = P // QUADS
+GROUP = 16
+LO = K_PASS // P
+LAST = H // P - 1
+M_BLOCKS = PICK // P
 HALF = PICK // 2
+W4, W2 = 0, 1
 
 
 def tile_list_mussel_relocation_scores_kernel(
     tc, tab_words, tab_scales, offs, offs2, offs3, offs4, w1, cap, page0, wgs, gain, w2, w4_words, w4_scales, bias, out
 ):
     nc = tc.nc
-    last = 2 * PACK - 1
     with ExitStack() as ctx:
         keep = ctx.enter_context(tc.tile_pool(name="keep", bufs=1))
         ring = ctx.enter_context(tc.tile_pool(name="ring", bufs=2))
         psum = ctx.enter_context(tc.psum_pool(name="psum", bufs=1))
-        ctx.enter_context(nc.allow_non_contiguous_dma(reason="per-row vectors, one value a partition"))
 
         def bank(number, shape, dtype, name):
             return psum.tile(shape, dtype, name=name, tag=f"bank{number}")
 
         tab_s = keep.tile([P, T], U8, name="tab_s", align_bytes=64)
         nc.vector.memset(tab_s[:].bitcast(I32), 0)
-        cap_lo = keep.tile([P, PACK], F32, name="cap_lo")
-        gain_lo = keep.tile([P, PACK], F32, name="gain_lo")
-        nc.gpsimd.dma_start(out=cap_lo[:], in_=cap[0:K_PASS].rearrange("(s p) -> p s", p=P))
-        nc.gpsimd.dma_start(out=gain_lo[:], in_=gain[0:K_PASS].rearrange("(s p) -> p s", p=P))
+        vec_rows = keep.tile([P, P], F32, name="vec_rows")
+        nc.gpsimd.memset(vec_rows[:], 0.0)
+        vectors = (cap[0:K_PASS], gain[0:K_PASS], bias)
+        for place, vector in enumerate(vectors):
+            nc.gpsimd.dma_start(
+                out=vec_rows[LO * place : LO * (place + 1), :], in_=vector.rearrange("(s p) -> s p", p=P)
+            )
         w4_s = keep.tile([P, R_PASSES, N], U8, name="w4_s", align_bytes=64)
-        nc.gpsimd.memset(w4_s[:].rearrange("p a n -> p (a n)").bitcast(I32), 0)
-        ident_bf = keep.tile([P, P], BF16, name="ident_bf")
+        nc.vector.memset(w4_s[:].rearrange("p a n -> p (a n)").bitcast(I32), 0)
         ident_f = keep.tile([P, P], F32, name="ident_f")
-        make_identity(nc, ident_bf[:])
+        ident_bf = keep.tile([P, P], BF16, name="ident_bf")
         make_identity(nc, ident_f[:])
+        make_identity(nc, ident_bf[:])
+        vec_turned = bank(4, [P, P], F32, "vec_turned")
+        nc.tensor.transpose(vec_turned[:], vec_rows[:], ident_f[:])
+        vec_cols = keep.tile([P, len(vectors) * LO], F32, name="vec_cols")
+        nc.scalar.copy(out=vec_cols[:], in_=vec_turned[:, 0 : len(vectors) * LO])
+        cap_lo = vec_cols[:, 0:LO]
+        gain_lo = vec_cols[:, LO : 2 * LO]
+        bias_cols = vec_cols[:, 2 * LO : 3 * LO]
 
         def load_list(source, name):
-            tile = keep.tile([P, S // 16], U16, name=name)
+            tile = keep.tile([P, S // GROUP], U16, name=name)
             nc.sync.dma_start(tile[:], source)
             return tile
 
@@ -72,10 +85,10 @@ def tile_list_mussel_relocation_scores_kernel(
 
         def load_page(s):
             tile = keep.tile([P, T2], F32, name=f"page{s}")
-            if s < PACK:
+            if s < LO:
                 source = page0[s * P : (s + 1) * P, :]
             else:
-                source = page0[K_PASS:H, :].rearrange("(p t) c -> t p c", t=PACK)[s - PACK]
+                source = page0[K_PASS:H, :].rearrange("(p t) c -> t p c", t=PACK)[s - LO]
             nc.sync.dma_start(out=tile[:], in_=source)
             return tile
 
@@ -90,59 +103,70 @@ def tile_list_mussel_relocation_scores_kernel(
 
         load_w1_lo(0)
         tab_w = [load_table(0)]
-        pick = load_list(offs, "pick")
+        pick_list = load_list(offs, "pick_list")
         tab_w.append(load_table(1))
-        rows = PACK * K_PASSES
+        scale_rows = PACK * K_PASSES
         for q in range(QUADS):
             nc.sync.dma_start(
-                out=tab_s[32 * q : 32 * q + rows, :].bitcast(I32),
+                out=tab_s[QUAD * q : QUAD * q + scale_rows, :].bitcast(I32),
                 in_=tab_scales[:, PACK * q : PACK * (q + 1), :].bitcast(I32),
             )
         tab_w.append(load_table(2))
         page = [load_page(0)]
-        old = load_list(offs4, "old")
-        put = load_list(offs2, "put")
+        old_list = load_list(offs4, "old_list")
+        put_list = load_list(offs2, "put_list")
         wgs_lo = keep.tile([P, S], F32, name="wgs_lo")
         nc.sync.dma_start(out=wgs_lo[:], in_=wgs)
-        new = load_list(offs3, "new")
-        for s in range(1, PACK):
+        load_w1_lo(1)
+        new_list = load_list(offs3, "new_list")
+        page.append(load_page(1))
+        for s in range(2, LO):
             load_w1_lo(s)
             page.append(load_page(s))
         w1_hi = [load_weight(w1, a, K_PASS, H, f"w1_hi{a}") for a in range(K_PASSES - 1)]
-        page.append(load_page(PACK))
-        w1_hi.append(load_weight(w1, K_PASSES - 1, K_PASS, H, "w1_hi2"))
+        page.append(load_page(LO))
+        w1_hi.append(load_weight(w1, K_PASSES - 1, K_PASS, H, f"w1_hi{K_PASSES - 1}"))
         cap_hi = keep.tile([P, PACK], F32, name="cap_hi")
         gain_hi = keep.tile([P, PACK], F32, name="gain_hi")
         nc.sync.dma_start(out=cap_hi[:], in_=cap[K_PASS:H].rearrange("(p t) -> p t", t=PACK))
         nc.sync.dma_start(out=gain_hi[:], in_=gain[K_PASS:H].rearrange("(p t) -> p t", t=PACK))
         w2_raw = [load_weight(w2, a, 0, N, f"w2_raw{a}") for a in range(R_PASSES)]
-        page.append(load_page(PACK + 1))
+        page.append(load_page(LO + 1))
         wgs_hi = keep.tile([P, PACK, S], F32, name="wgs_hi")
         for q in (0, 2, 1, 3):
             nc.sync.dma_start(
-                out=wgs_hi[32 * q : 32 * (q + 1)].rearrange("p t j -> p (t j)"),
+                out=wgs_hi[QUAD * q : QUAD * (q + 1)].rearrange("p t j -> p (t j)"),
                 in_=wgs.rearrange("(p t) j -> p (t j)", t=PACK),
             )
-        for s in range(PACK + 2, 2 * PACK):
+        for s in range(LO + 2, LAST + 1):
             page.append(load_page(s))
         w4_w = keep.tile([P, R_PASSES, 2 * N], U8, name="w4_w", align_bytes=64)
         nc.sync.dma_start(out=w4_w[:].bitcast(I32), in_=w4_words.rearrange("a p c -> p a c").bitcast(I32))
         for q in range(QUADS):
             nc.sync.dma_start(
-                out=w4_s[32 * q : 32 * q + PACK].bitcast(I32),
+                out=w4_s[QUAD * q : QUAD * q + PACK].bitcast(I32),
                 in_=w4_scales[:, PACK * q : PACK * (q + 1), :].rearrange("a r n -> r a n").bitcast(I32),
             )
-        bias_c = keep.tile([P, N_BLOCKS], F32, name="bias_c")
-        nc.sync.dma_start(out=bias_c[:], in_=bias.rearrange("(b p) -> p b", p=P))
 
         v_s = keep.tile([P, S], U8, name="v_s", align_bytes=64)
         v_w = []
         for a in range(K_PASSES):
+            if a == K_PASSES - 1:
+                nc.vector.tensor_copy(v_s[:], tab_s[:].indirect(pick_list[:]))
             words = keep.tile([P, S], U32, name=f"v_w{a}", align_bytes=64)
-            nc.vector.tensor_copy(words[:], tab_w[a][:].bitcast(U32).indirect(pick[:]))
+            nc.vector.tensor_copy(words[:], tab_w[a][:].bitcast(U32).indirect(pick_list[:]))
             v_w.append(words)
-            if a == 1:
-                nc.vector.tensor_copy(v_s[:], tab_s[:].indirect(pick[:]))
+
+        def stage_tag(s):
+            if s <= LO:
+                return f"lo_raw{s % LO}"
+            return f"hi_grouped{s}"
+
+        h_tags = ["h_a", "h_b"] * 3 + ["h_c", "h_a"]
+        old_tags = {0: "old0", LO + 1: stage_tag(LO - 1), LO + 2: stage_tag(LO), LAST: stage_tag(LO - 1)}
+        change_tags = {LO: "change_a", LO + 1: "change_b", LO + 2: stage_tag(LO + 1), LAST: stage_tag(LO + 2)}
+        w2_tags = [change_tags[LO], change_tags[LAST]]
+        x_tags = [change_tags[LAST - 1], h_tags[LAST - 1]]
 
         def interleave(grouped, raw):
             nc.scalar.copy(
@@ -153,207 +177,192 @@ def tile_list_mussel_relocation_scores_kernel(
         def quantize(codes, scales, grouped):
             nc.vector.quantize_mx(out=codes.bitcast(FP8X4), scales=scales, in_=grouped)
 
+        w1_grouped = {}
         w1_c = {}
         w1_s = {}
 
-        w1_g = {}
-        h_tags = ["h_a", "h_b", "h_a", "h_b", "h_a", "h_b", "h_c", "h_a"]
-
-        def stage_tag(s):
-            if s <= PACK:
-                return f"lo_raw{s % PACK}"
-            return f"hi_grouped{s}"
-
         def round_w1(s):
-            if s < PACK:
+            if s < LO:
                 grouped = ring.tile([P, K_PASSES, P * PACK], BF16, name="w1_grouped", align_bytes=64)[:]
             else:
                 grouped = keep.tile(
                     [P, K_PASSES, P * PACK], BF16, name=f"w1_grouped{s}", tag=stage_tag(s), align_bytes=64
                 )[:]
             for a in range(K_PASSES):
-                if s < PACK:
+                if s < LO:
                     interleave(grouped[:, a, :], w1_lo[s][:, a])
                 else:
                     nc.scalar.copy(
-                        out=grouped[:, a, :].rearrange("p (m j) -> p m j", j=PACK),
-                        in_=w1_hi[a][:].rearrange("p j (m t) -> p t m j", t=PACK)[:, s - PACK],
+                        out=grouped[:, a, :].rearrange("p (c j) -> p c j", j=PACK),
+                        in_=w1_hi[a][:].rearrange("p j (c t) -> p t c j", t=PACK)[:, s - LO],
                     )
-            w1_g[s] = grouped
+            w1_grouped[s] = grouped
 
         def quantize_w1(s):
-            grouped = w1_g[s]
-            tag = f"w1_c{s}" if s < last - 1 else h_tags[s - 2]
+            grouped = w1_grouped[s]
+            tag = f"w1_c{s}" if s < LAST - 1 else h_tags[s - 2]
             codes = keep.tile([P, K_PASSES, P], U32, name=f"w1_c{s}", tag=tag, align_bytes=64)
             scales = keep.tile([P, K_PASSES, P], U8, name=f"w1_s{s}", align_bytes=64)
-            for a in range(K_PASSES):
-                if s <= PACK:
+            if s <= LO:
+                for a in range(K_PASSES):
                     quantize(codes[:, a, :], scales[:, a, :], grouped[:, a, :])
-                w1_c[s, a] = codes[:, a, :]
-                w1_s[s, a] = scales[:, a, :]
-            if s > PACK:
+            else:
                 quantize(
                     codes[:].rearrange("p a c -> p (a c)"),
                     scales[:].rearrange("p a c -> p (a c)"),
                     grouped.rearrange("p a c -> p (a c)"),
                 )
+            w1_c[s] = codes
+            w1_s[s] = scales
 
-        h_banks = [0, 1, 2, 3]
-        sums = {}
+        h_sums = {}
 
         def first_product(s):
-            acc = bank(h_banks[s % 4], [P, S], F32, f"h_sum{s}")
+            acc = bank(s % LO, [P, S], F32, f"h_sum{s}")
             for a in range(K_PASSES):
                 nc.tensor.matmul_mx(
                     out=acc[:],
-                    lhsT=w1_c[s, a].bitcast(FP8X4),
-                    lhsT_scale=w1_s[s, a],
+                    lhsT=w1_c[s][:, a, :].bitcast(FP8X4),
+                    lhsT_scale=w1_s[s][:, a, :],
                     rhs=v_w[a][:].bitcast(FP8X4),
                     rhs_scale=v_s[PACK * a : P, :],
                     start=(a == 0),
                     stop=(a == K_PASSES - 1),
                 )
-            sums[s] = acc
+            h_sums[s] = acc
 
-        capped = {}
+        weighted = {}
 
-        def cap_rows(s):
-            h = keep.tile([P, S], F32, name=f"h{s}", tag=h_tags[s], align_bytes=64)
-            limit = cap_lo[:, s : s + 1] if s < PACK else cap_hi[:, s - PACK : s - PACK + 1]
-            weights = wgs_lo[:] if s < PACK else wgs_hi[:, s - PACK, :]
+        def cap_and_weigh(s):
+            values = keep.tile([P, S], F32, name=f"h{s}", tag=h_tags[s], align_bytes=64)
+            limit = cap_lo[:, s : s + 1] if s < LO else cap_hi[:, s - LO : s - LO + 1]
+            weights = wgs_lo[:] if s < LO else wgs_hi[:, s - LO, :]
             nc.vector.scalar_tensor_tensor(
-                out=h[:], in0=sums[s][:], scalar=limit, in1=weights, op0=ALU.min, op1=ALU.mult
+                out=values[:], in0=h_sums[s][:], scalar=limit, in1=weights, op0=ALU.min, op1=ALU.mult
             )
-            capped[s] = h
+            weighted[s] = values
 
         olds = {}
         changes = {}
-        old_tags = {0: "old0", 5: stage_tag(3), 6: stage_tag(4), 7: stage_tag(3)}
-        change_tags = {4: "change4", 5: "change5", 6: stage_tag(5), 7: stage_tag(6)}
-
-        def make_room(s):
-            if 1 <= s <= PACK:
-                pair = keep.tile([P, 2, PICK], F32, name=f"picked{s}", tag=stage_tag(s), align_bytes=64)
-                olds[s] = pair[:, 0, :]
-                changes[s - 1] = pair[:, 1, :]
-            else:
-                olds[s] = keep.tile([P, PICK], F32, name=f"old{s}", tag=old_tags[s], align_bytes=64)[:]
-
-        def earlier(s):
-            return olds[s]
-
-        def change(s):
-            if s not in changes:
-                changes[s] = keep.tile([P, PICK], F32, name=f"change{s}", tag=change_tags[s], align_bytes=64)[:]
-            return changes[s]
 
         def fetch_old(s):
-            make_room(s)
-            nc.vector.tensor_copy(earlier(s), page[s][:].indirect(old[:]))
+            if 1 <= s <= LO:
+                both = keep.tile([P, 2, PICK], F32, name=f"picked{s}", tag=stage_tag(s), align_bytes=64)
+                olds[s] = both[:, 0, :]
+                changes[s - 1] = both[:, 1, :]
+            else:
+                olds[s] = keep.tile([P, PICK], F32, name=f"old{s}", tag=old_tags[s], align_bytes=64)[:]
+            nc.vector.tensor_copy(olds[s], page[s][:].indirect(old_list[:]))
 
         def put_new(s):
-            nc.vector.tensor_copy(page[s][:].indirect(put[:]), capped[s][:])
+            nc.vector.tensor_copy(page[s][:].indirect(put_list[:]), weighted[s][:])
 
         def fetch_new(s, m0, m1):
+            if s not in changes:
+                changes[s] = keep.tile([P, PICK], F32, name=f"change{s}", tag=change_tags[s], align_bytes=64)[:]
             nc.vector.tensor_tensor(
-                change(s)[:, m0:m1], page[s][:].indirect(new[:, m0 // 16 : m1 // 16]), earlier(s)[:, m0:m1], ALU.subtract
+                changes[s][:, m0:m1],
+                page[s][:].indirect(new_list[:, m0 // GROUP : m1 // GROUP]),
+                olds[s][:, m0:m1],
+                ALU.subtract,
             )
 
-        x_t = keep.tile([P, PICK // P, K_PASS], BF16, name="x_t")
+        x_turned = keep.tile([P, M_BLOCKS, K_PASS], BF16, name="x_turned")
         x_hi = keep.tile([P, PACK, PICK], BF16, name="x_hi")
         x_lo = {}
 
-        def finish(s, m0, m1):
-            if s < PACK:
+        def make_x(s, m0, m1):
+            if s < LO:
                 x_lo[s] = keep.tile([P, PICK], BF16, name=f"x_lo{s}", tag=f"w1_c{s + 1}", align_bytes=64)
                 x, factor = x_lo[s][:], gain_lo[:, s : s + 1]
             else:
-                x, factor = x_hi[:, s - PACK, :], gain_hi[:, s - PACK : s - PACK + 1]
+                x, factor = x_hi[:, s - LO, :], gain_hi[:, s - LO : s - LO + 1]
             nc.vector.scalar_tensor_tensor(
                 out=x[:, m0:m1],
-                in0=earlier(s)[:, m0:m1],
+                in0=olds[s][:, m0:m1],
                 scalar=factor,
-                in1=change(s)[:, m0:m1],
+                in1=changes[s][:, m0:m1],
                 op0=ALU.mult,
                 op1=ALU.max,
             )
 
-        def turn_lo(pair):
-            turned = bank(pair, [P, 2, PICK // P, P], BF16, f"turned{pair}")
+        def turn_lo(two):
+            turned = bank(two, [P, 2, M_BLOCKS, P], BF16, f"turned{two}")
             for i in range(2):
-                for mb in range(PICK // P):
-                    nc.tensor.transpose(turned[:, i, mb, :], x_lo[2 * pair + i][:, mb * P : (mb + 1) * P], ident_bf[:])
+                for mb in range(M_BLOCKS):
+                    nc.tensor.transpose(turned[:, i, mb, :], x_lo[2 * two + i][:, mb * P : (mb + 1) * P], ident_bf[:])
             nc.scalar.copy(
-                out=x_t[:, :, 2 * pair * P : 2 * (pair + 1) * P].rearrange("p b (i r) -> p i b r", i=2), in_=turned[:]
+                out=x_turned[:, :, 2 * two * P : 2 * (two + 1) * P].rearrange("p b (i r) -> p i b r", i=2),
+                in_=turned[:],
             )
 
-        x_g = [keep.tile([P, PICK, PACK], BF16, name=f"x_g{b}", align_bytes=64) for b in range(R_PASSES)]
+        x_grouped = [keep.tile([P, PICK, PACK], BF16, name=f"x_g{b}", align_bytes=64) for b in range(R_PASSES)]
         x_c = {}
         x_s = [keep.tile([P, PICK], U8, name=f"x_s{b}", align_bytes=64) for b in range(R_PASSES)]
 
         def regroup_lo():
-            target = x_g[0][:].rearrange("p m t -> p (m t)").bitcast(F32)
-            for pair in range(2):
-                back = bank(4 + pair, [P, 2, 2, P], F32, f"back{pair}")
+            target = x_grouped[0][:].rearrange("p m t -> p (m t)").bitcast(F32)
+            for two in range(M_BLOCKS // 2):
+                back = bank(4 + two, [P, 2, 2, P], F32, f"back{two}")
                 for i in range(2):
-                    words = x_t[:, 2 * pair + i, :].bitcast(F32)
+                    words = x_turned[:, 2 * two + i, :].bitcast(F32)
                     for u in range(2):
                         nc.tensor.transpose(back[:, i, u, :], words[:, u : 2 * P : 2], ident_f[:])
                 nc.scalar.copy(
-                    out=target[:, pair * 4 * P : (pair + 1) * 4 * P].rearrange("p (i m u) -> p i m u", i=2, u=2),
+                    out=target[:, two * 4 * P : (two + 1) * 4 * P].rearrange("p (i m u) -> p i m u", i=2, u=2),
                     in_=back[:].rearrange("p i u m -> p i m u"),
                 )
 
-        def quantize_x(b, m0, m1):
-            if b not in x_c:
-                x_c[b] = keep.tile([P, PICK], U32, name=f"x_c{b}", tag=[change_tags[last - 1], "h_c"][b], align_bytes=64)
-            quantize(x_c[b][:, m0:m1], x_s[b][:, m0:m1], x_g[b][:, m0:m1, :].rearrange("p m t -> p (m t)"))
-
         def regroup_hi(copy, m0, m1):
             copy(
-                x_g[1][:, m0:m1, :].rearrange("p (c i) t -> p c t i", i=PACK),
+                x_grouped[1][:, m0:m1, :].rearrange("p (c i) t -> p c t i", i=PACK),
                 x_hi[:, :, m0:m1].rearrange("p t (c i) -> p c t i", i=PACK),
             )
 
+        def quantize_x(b, m0, m1):
+            if b not in x_c:
+                x_c[b] = keep.tile([P, PICK], U32, name=f"x_c{b}", tag=x_tags[b], align_bytes=64)
+            quantize(x_c[b][:, m0:m1], x_s[b][:, m0:m1], x_grouped[b][:, m0:m1, :].rearrange("p m t -> p (m t)"))
+
+        w2_grouped = []
         w2_c = []
         w2_s = []
 
-        w2_g = []
-
-        def round_w2(a):
+        def round_w2(b):
             grouped = ring.tile([P, N * PACK], BF16, name="w2_grouped", align_bytes=64)
-            interleave(grouped[:], w2_raw[a][:])
-            w2_g.append(grouped)
+            interleave(grouped[:], w2_raw[b][:])
+            w2_grouped.append(grouped)
 
-        def quantize_w2(a):
-            codes = keep.tile([P, N], U32, name=f"w2_c{a}", tag=change_tags[PACK + a], align_bytes=64)
-            scales = keep.tile([P, N], U8, name=f"w2_s{a}", align_bytes=64)
-            quantize(codes[:], scales[:], w2_g[a][:])
+        def quantize_w2(b):
+            codes = keep.tile([P, N], U32, name=f"w2_c{b}", tag=w2_tags[b], align_bytes=64)
+            scales = keep.tile([P, N], U8, name=f"w2_s{b}", align_bytes=64)
+            quantize(codes[:], scales[:], w2_grouped[b][:])
             w2_c.append(codes)
             w2_s.append(scales)
 
-        y_banks = {}
+        first_bank = {(0, W4): 6, (0, W2): 4, (1, W4): 0, (1, W2): 2}
+        scores = {}
 
         def open_scores(half):
-            for kind in range(2):
+            for kind in (W4, W2):
                 for pair in range(2):
-                    number = [[6, 4], [0, 2]][half][kind] + pair
-                    y_banks[half, kind, pair] = bank(number, [P, 2, HALF], F32, f"y{half}{kind}{pair}")
+                    number = first_bank[half, kind] + pair
+                    scores[half, kind, pair] = bank(number, [P, 2, HALF], F32, f"y{half}{kind}{pair}")
 
         def second_pass(half, b):
             cols = slice(half * HALF, (half + 1) * HALF)
             for pair in range(2):
-                for kind in range(2):
+                for kind in (W4, W2):
                     for i in range(2):
                         nb = 2 * pair + i
-                        if kind == 0:
+                        if kind == W4:
                             codes = w4_w[:, b, 2 * P * nb : 2 * P * (nb + 1)].bitcast(FP4X4)
                             scales = w4_s[:, b, P * nb : P * (nb + 1)]
                         else:
                             codes = w2_c[b][:, P * nb : P * (nb + 1)].bitcast(FP8X4)
                             scales = w2_s[b][:, P * nb : P * (nb + 1)]
                         nc.tensor.matmul_mx(
-                            out=y_banks[half, kind, pair][:, i, :],
+                            out=scores[half, kind, pair][:, i, :],
                             lhsT=codes,
                             lhsT_scale=scales,
                             rhs=x_c[b][:, cols].bitcast(FP8X4),
@@ -370,70 +379,72 @@ def tile_list_mussel_relocation_scores_kernel(
                     nb = 2 * pair + i
                     nc.scalar.activation(
                         out=y4[:, i, :],
-                        in_=y_banks[half, 0, pair][:, i, :],
+                        in_=scores[half, W4, pair][:, i, :],
                         func=ACT.Identity,
-                        bias=bias_c[:, nb : nb + 1],
+                        bias=bias_cols[:, nb : nb + 1],
                     )
                     nc.vector.scalar_tensor_tensor(
                         out=result[:, i, :],
-                        in0=y_banks[half, 1, pair][:, i, :],
-                        scalar=bias_c[:, nb : nb + 1],
+                        in0=scores[half, W2, pair][:, i, :],
+                        scalar=bias_cols[:, nb : nb + 1],
                         in1=y4[:, i, :],
                         op0=ALU.add,
                         op1=ALU.min,
                     )
-                target = out[pair * 2 * P : (pair + 1) * 2 * P, half * HALF : (half + 1) * HALF]
-                nc.sync.dma_start(out=target.rearrange("(i p) m -> p i m", p=P), in_=result[:])
+                    target = out[nb * P : (nb + 1) * P, half * HALF : (half + 1) * HALF]
+                    nc.sync.dma_start(out=target, in_=result[:, i, :])
 
         round_w1(0)
         quantize_w1(0)
         first_product(0)
         fetch_old(0)
-        cap_rows(0)
-        for s in range(PACK):
+        cap_and_weigh(0)
+        for s in range(LO):
             put_new(s)
             round_w1(s + 1)
             quantize_w1(s + 1)
             first_product(s + 1)
             fetch_old(s + 1)
             fetch_new(s, 0, PICK)
-            cap_rows(s + 1)
-            finish(s, 0, PICK)
-        for s in range(PACK + 1, 2 * PACK):
+            cap_and_weigh(s + 1)
+            make_x(s, 0, PICK)
+        for s in range(LO + 1, LAST + 1):
             round_w1(s)
-        for a in range(R_PASSES):
-            round_w2(a)
-        quantize_w1(PACK + 1)
-        first_product(PACK + 1)
-        cap_rows(PACK + 1)
-        for pair in range(2):
-            turn_lo(pair)
+        for b in range(R_PASSES):
+            round_w2(b)
+        quantize_w1(LO + 1)
+        first_product(LO + 1)
+        cap_and_weigh(LO + 1)
+        for two in range(LO // 2):
+            turn_lo(two)
         regroup_lo()
-        for s in range(PACK, last):
+        for s in range(LO, LAST):
             put_new(s)
             fetch_old(s + 1)
             fetch_new(s, 0, PICK)
-            if s > PACK:
-                cap_rows(s + 1)
-            if s + 2 <= last:
+            if s > LO:
+                cap_and_weigh(s + 1)
+            if s + 2 <= LAST:
                 quantize_w1(s + 2)
                 first_product(s + 2)
-            finish(s, 0, PICK)
-            if s > PACK:
-                quantize_w2(s - PACK - 1)
-        put_new(last)
+            make_x(s, 0, PICK)
+            if s + 2 == LAST:
+                quantize_w2(0)
+        put_new(LAST)
         quantize_x(0, 0, PICK)
         for half in range(2):
             open_scores(half)
             second_pass(half, 0)
-        fetch_new(last, 0, HALF)
-        fetch_new(last, HALF, PICK)
-        finish(last, 0, HALF)
+        fetch_new(LAST, 0, HALF)
+        fetch_new(LAST, HALF, PICK)
+        make_x(LAST, 0, HALF)
         regroup_hi(nc.scalar.copy, 0, HALF)
-        finish(last, HALF, PICK)
+        make_x(LAST, HALF, PICK)
         regroup_hi(nc.vector.tensor_copy, HALF, PICK)
-        for half in range(2):
-            quantize_x(1, half * HALF, (half + 1) * HALF)
-            second_pass(half, 1)
+        quantize_x(1, 0, HALF)
+        quantize_w2(1)
+        second_pass(0, 1)
+        quantize_x(1, HALF, PICK)
+        second_pass(1, 1)
         for half in range(2):
             scores_out(half)

from contextlib import ExitStack

import concourse.mybir as mybir
from concourse.masks import make_identity

K, T, S, T2, PICK, H, N = 1536, 2048, 512, 1024, 512, 1024, 512
FLOPS = 2 * K * H * S + 2 * 2 * H * N * PICK

F32 = mybir.dt.float32
BF16 = mybir.dt.bfloat16
I32 = mybir.dt.int32
U32 = mybir.dt.uint32
U16 = mybir.dt.uint16
U8 = mybir.dt.uint8
FP8X4 = mybir.dt.float8_e4m3fn_x4
FP4X4 = mybir.dt.float4_e2m1fn_x4
ALU = mybir.AluOpType
ACT = mybir.ActivationFunctionType

P = 128
PACK = 4
K_PASS = P * PACK
K_PASSES = K // K_PASS
R_PASSES = H // K_PASS
QUADS = 4
QUAD = P // QUADS
GROUP = 16
LO = K_PASS // P
LAST = H // P - 1
M_BLOCKS = PICK // P
HALF = PICK // 2
W4, W2 = 0, 1


def tile_list_mussel_relocation_scores_kernel(
    tc, tab_words, tab_scales, offs, offs2, offs3, offs4, w1, cap, page0, wgs, gain, w2, w4_words, w4_scales, bias, out
):
    nc = tc.nc
    with ExitStack() as ctx:
        keep = ctx.enter_context(tc.tile_pool(name="keep", bufs=1))
        ring = ctx.enter_context(tc.tile_pool(name="ring", bufs=2))
        psum = ctx.enter_context(tc.psum_pool(name="psum", bufs=1))

        def bank(number, shape, dtype, name):
            return psum.tile(shape, dtype, name=name, tag=f"bank{number}")

        tab_s = keep.tile([P, T], U8, name="tab_s", align_bytes=64)
        nc.vector.memset(tab_s[:].bitcast(I32), 0)
        vec_rows = keep.tile([P, P], F32, name="vec_rows")
        nc.gpsimd.memset(vec_rows[:], 0.0)
        vectors = (cap[0:K_PASS], gain[0:K_PASS], bias)
        for place, vector in enumerate(vectors):
            nc.gpsimd.dma_start(
                out=vec_rows[LO * place : LO * (place + 1), :], in_=vector.rearrange("(s p) -> s p", p=P)
            )
        w4_s = keep.tile([P, R_PASSES, N], U8, name="w4_s", align_bytes=64)
        nc.vector.memset(w4_s[:].rearrange("p a n -> p (a n)").bitcast(I32), 0)
        ident_f = keep.tile([P, P], F32, name="ident_f")
        ident_bf = keep.tile([P, P], BF16, name="ident_bf")
        make_identity(nc, ident_f[:])
        make_identity(nc, ident_bf[:])
        vec_turned = bank(4, [P, P], F32, "vec_turned")
        nc.tensor.transpose(vec_turned[:], vec_rows[:], ident_f[:])
        vec_cols = keep.tile([P, len(vectors) * LO], F32, name="vec_cols")
        nc.scalar.copy(out=vec_cols[:], in_=vec_turned[:, 0 : len(vectors) * LO])
        cap_lo = vec_cols[:, 0:LO]
        gain_lo = vec_cols[:, LO : 2 * LO]
        bias_cols = vec_cols[:, 2 * LO : 3 * LO]

        def load_list(source, name):
            tile = keep.tile([P, S // GROUP], U16, name=name)
            nc.sync.dma_start(tile[:], source)
            return tile

        def load_table(a):
            tile = keep.tile([P, T], I32, name=f"tab_w{a}", align_bytes=64)
            nc.sync.dma_start(out=tile[:], in_=tab_words[a].rearrange("p t i -> p (t i)").bitcast(I32))
            return tile

        def load_weight(weight, a, c0, c1, name):
            tile = keep.tile([P, PACK, c1 - c0], F32, name=name)
            source = weight[a * K_PASS : (a + 1) * K_PASS, c0:c1]
            nc.sync.dma_start(out=tile[:], in_=source.rearrange("(p j) c -> p j c", j=PACK))
            return tile

        def load_page(s):
            tile = keep.tile([P, T2], F32, name=f"page{s}")
            if s < LO:
                source = page0[s * P : (s + 1) * P, :]
            else:
                source = page0[K_PASS:H, :].rearrange("(p t) c -> t p c", t=PACK)[s - LO]
            nc.sync.dma_start(out=tile[:], in_=source)
            return tile

        w1_lo = {}

        def load_w1_lo(s):
            raw = keep.tile([P, K_PASSES, PACK, P], F32, name=f"w1_lo{s}", tag=f"lo_raw{s}", align_bytes=64)
            for a in range(K_PASSES):
                source = w1[a * K_PASS : (a + 1) * K_PASS, s * P : (s + 1) * P]
                nc.sync.dma_start(out=raw[:, a], in_=source.rearrange("(p j) c -> p j c", j=PACK))
            w1_lo[s] = raw

        load_w1_lo(0)
        tab_w = [load_table(0)]
        pick_list = load_list(offs, "pick_list")
        tab_w.append(load_table(1))
        scale_rows = PACK * K_PASSES
        for q in range(QUADS):
            nc.sync.dma_start(
                out=tab_s[QUAD * q : QUAD * q + scale_rows, :].bitcast(I32),
                in_=tab_scales[:, PACK * q : PACK * (q + 1), :].bitcast(I32),
            )
        tab_w.append(load_table(2))
        page = [load_page(0)]
        old_list = load_list(offs4, "old_list")
        put_list = load_list(offs2, "put_list")
        wgs_lo = keep.tile([P, S], F32, name="wgs_lo")
        nc.sync.dma_start(out=wgs_lo[:], in_=wgs)
        load_w1_lo(1)
        new_list = load_list(offs3, "new_list")
        page.append(load_page(1))
        for s in range(2, LO):
            load_w1_lo(s)
            page.append(load_page(s))
        w1_hi = [load_weight(w1, a, K_PASS, H, f"w1_hi{a}") for a in range(K_PASSES - 1)]
        page.append(load_page(LO))
        w1_hi.append(load_weight(w1, K_PASSES - 1, K_PASS, H, f"w1_hi{K_PASSES - 1}"))
        cap_hi = keep.tile([P, PACK], F32, name="cap_hi")
        gain_hi = keep.tile([P, PACK], F32, name="gain_hi")
        nc.sync.dma_start(out=cap_hi[:], in_=cap[K_PASS:H].rearrange("(p t) -> p t", t=PACK))
        nc.sync.dma_start(out=gain_hi[:], in_=gain[K_PASS:H].rearrange("(p t) -> p t", t=PACK))
        w2_raw = [load_weight(w2, a, 0, N, f"w2_raw{a}") for a in range(R_PASSES)]
        page.append(load_page(LO + 1))
        wgs_hi = keep.tile([P, PACK, S], F32, name="wgs_hi")
        for q in (0, 2, 1, 3):
            nc.sync.dma_start(
                out=wgs_hi[QUAD * q : QUAD * (q + 1)].rearrange("p t j -> p (t j)"),
                in_=wgs.rearrange("(p t) j -> p (t j)", t=PACK),
            )
        for s in range(LO + 2, LAST + 1):
            page.append(load_page(s))
        w4_w = keep.tile([P, R_PASSES, 2 * N], U8, name="w4_w", align_bytes=64)
        nc.sync.dma_start(out=w4_w[:].bitcast(I32), in_=w4_words.rearrange("a p c -> p a c").bitcast(I32))
        for q in range(QUADS):
            nc.sync.dma_start(
                out=w4_s[QUAD * q : QUAD * q + PACK].bitcast(I32),
                in_=w4_scales[:, PACK * q : PACK * (q + 1), :].rearrange("a r n -> r a n").bitcast(I32),
            )

        v_s = keep.tile([P, S], U8, name="v_s", align_bytes=64)
        v_w = []
        for a in range(K_PASSES):
            if a == K_PASSES - 1:
                nc.vector.tensor_copy(v_s[:], tab_s[:].indirect(pick_list[:]))
            words = keep.tile([P, S], U32, name=f"v_w{a}", align_bytes=64)
            nc.vector.tensor_copy(words[:], tab_w[a][:].bitcast(U32).indirect(pick_list[:]))
            v_w.append(words)

        def stage_tag(s):
            if s <= LO:
                return f"lo_raw{s % LO}"
            return f"hi_grouped{s}"

        h_tags = ["h_a", "h_b"] * 3 + ["h_c", "h_a"]
        old_tags = {0: "old0", LO + 1: stage_tag(LO - 1), LO + 2: stage_tag(LO), LAST: stage_tag(LO - 1)}
        change_tags = {LO: "change_a", LO + 1: "change_b", LO + 2: stage_tag(LO + 1), LAST: stage_tag(LO + 2)}
        w2_tags = [change_tags[LO], change_tags[LAST]]
        x_tags = [change_tags[LAST - 1], h_tags[LAST - 1]]

        def interleave(grouped, raw):
            nc.scalar.copy(
                out=grouped.rearrange("p (c i j) -> p c j i", i=PACK, j=PACK),
                in_=raw.rearrange("p j (c i) -> p c j i", i=PACK),
            )

        def quantize(codes, scales, grouped):
            nc.vector.quantize_mx(out=codes.bitcast(FP8X4), scales=scales, in_=grouped)

        w1_grouped = {}
        w1_c = {}
        w1_s = {}

        def round_w1(s):
            if s < LO:
                grouped = ring.tile([P, K_PASSES, P * PACK], BF16, name="w1_grouped", align_bytes=64)[:]
            else:
                grouped = keep.tile(
                    [P, K_PASSES, P * PACK], BF16, name=f"w1_grouped{s}", tag=stage_tag(s), align_bytes=64
                )[:]
            for a in range(K_PASSES):
                if s < LO:
                    interleave(grouped[:, a, :], w1_lo[s][:, a])
                else:
                    nc.scalar.copy(
                        out=grouped[:, a, :].rearrange("p (c j) -> p c j", j=PACK),
                        in_=w1_hi[a][:].rearrange("p j (c t) -> p t c j", t=PACK)[:, s - LO],
                    )
            w1_grouped[s] = grouped

        def quantize_w1(s):
            grouped = w1_grouped[s]
            tag = f"w1_c{s}" if s < LAST - 1 else h_tags[s - 2]
            codes = keep.tile([P, K_PASSES, P], U32, name=f"w1_c{s}", tag=tag, align_bytes=64)
            scales = keep.tile([P, K_PASSES, P], U8, name=f"w1_s{s}", align_bytes=64)
            if s <= LO:
                for a in range(K_PASSES):
                    quantize(codes[:, a, :], scales[:, a, :], grouped[:, a, :])
            else:
                quantize(
                    codes[:].rearrange("p a c -> p (a c)"),
                    scales[:].rearrange("p a c -> p (a c)"),
                    grouped.rearrange("p a c -> p (a c)"),
                )
            w1_c[s] = codes
            w1_s[s] = scales

        h_sums = {}

        def first_product(s):
            acc = bank(s % LO, [P, S], F32, f"h_sum{s}")
            for a in range(K_PASSES):
                nc.tensor.matmul_mx(
                    out=acc[:],
                    lhsT=w1_c[s][:, a, :].bitcast(FP8X4),
                    lhsT_scale=w1_s[s][:, a, :],
                    rhs=v_w[a][:].bitcast(FP8X4),
                    rhs_scale=v_s[PACK * a : P, :],
                    start=(a == 0),
                    stop=(a == K_PASSES - 1),
                )
            h_sums[s] = acc

        weighted = {}

        def cap_and_weigh(s):
            values = keep.tile([P, S], F32, name=f"h{s}", tag=h_tags[s], align_bytes=64)
            limit = cap_lo[:, s : s + 1] if s < LO else cap_hi[:, s - LO : s - LO + 1]
            weights = wgs_lo[:] if s < LO else wgs_hi[:, s - LO, :]
            nc.vector.scalar_tensor_tensor(
                out=values[:], in0=h_sums[s][:], scalar=limit, in1=weights, op0=ALU.min, op1=ALU.mult
            )
            weighted[s] = values

        olds = {}
        changes = {}

        def fetch_old(s):
            if 1 <= s <= LO:
                both = keep.tile([P, 2, PICK], F32, name=f"picked{s}", tag=stage_tag(s), align_bytes=64)
                olds[s] = both[:, 0, :]
                changes[s - 1] = both[:, 1, :]
            else:
                olds[s] = keep.tile([P, PICK], F32, name=f"old{s}", tag=old_tags[s], align_bytes=64)[:]
            nc.vector.tensor_copy(olds[s], page[s][:].indirect(old_list[:]))

        def put_new(s):
            nc.vector.tensor_copy(page[s][:].indirect(put_list[:]), weighted[s][:])

        def fetch_new(s, m0, m1):
            if s not in changes:
                changes[s] = keep.tile([P, PICK], F32, name=f"change{s}", tag=change_tags[s], align_bytes=64)[:]
            nc.vector.tensor_tensor(
                changes[s][:, m0:m1],
                page[s][:].indirect(new_list[:, m0 // GROUP : m1 // GROUP]),
                olds[s][:, m0:m1],
                ALU.subtract,
            )

        x_turned = keep.tile([P, M_BLOCKS, K_PASS], BF16, name="x_turned")
        x_hi = keep.tile([P, PACK, PICK], BF16, name="x_hi")
        x_lo = {}

        def make_x(s, m0, m1):
            if s < LO:
                x_lo[s] = keep.tile([P, PICK], BF16, name=f"x_lo{s}", tag=f"w1_c{s + 1}", align_bytes=64)
                x, factor = x_lo[s][:], gain_lo[:, s : s + 1]
            else:
                x, factor = x_hi[:, s - LO, :], gain_hi[:, s - LO : s - LO + 1]
            nc.vector.scalar_tensor_tensor(
                out=x[:, m0:m1],
                in0=olds[s][:, m0:m1],
                scalar=factor,
                in1=changes[s][:, m0:m1],
                op0=ALU.mult,
                op1=ALU.max,
            )

        def turn_lo(two):
            turned = bank(two, [P, 2, M_BLOCKS, P], BF16, f"turned{two}")
            for i in range(2):
                for mb in range(M_BLOCKS):
                    nc.tensor.transpose(turned[:, i, mb, :], x_lo[2 * two + i][:, mb * P : (mb + 1) * P], ident_bf[:])
            nc.scalar.copy(
                out=x_turned[:, :, 2 * two * P : 2 * (two + 1) * P].rearrange("p b (i r) -> p i b r", i=2),
                in_=turned[:],
            )

        x_grouped = [keep.tile([P, PICK, PACK], BF16, name=f"x_g{b}", align_bytes=64) for b in range(R_PASSES)]
        x_c = {}
        x_s = [keep.tile([P, PICK], U8, name=f"x_s{b}", align_bytes=64) for b in range(R_PASSES)]

        def regroup_lo():
            target = x_grouped[0][:].rearrange("p m t -> p (m t)").bitcast(F32)
            for two in range(M_BLOCKS // 2):
                back = bank(4 + two, [P, 2, 2, P], F32, f"back{two}")
                for i in range(2):
                    words = x_turned[:, 2 * two + i, :].bitcast(F32)
                    for u in range(2):
                        nc.tensor.transpose(back[:, i, u, :], words[:, u : 2 * P : 2], ident_f[:])
                nc.scalar.copy(
                    out=target[:, two * 4 * P : (two + 1) * 4 * P].rearrange("p (i m u) -> p i m u", i=2, u=2),
                    in_=back[:].rearrange("p i u m -> p i m u"),
                )

        def regroup_hi(copy, m0, m1):
            copy(
                x_grouped[1][:, m0:m1, :].rearrange("p (c i) t -> p c t i", i=PACK),
                x_hi[:, :, m0:m1].rearrange("p t (c i) -> p c t i", i=PACK),
            )

        def quantize_x(b, m0, m1):
            if b not in x_c:
                x_c[b] = keep.tile([P, PICK], U32, name=f"x_c{b}", tag=x_tags[b], align_bytes=64)
            quantize(x_c[b][:, m0:m1], x_s[b][:, m0:m1], x_grouped[b][:, m0:m1, :].rearrange("p m t -> p (m t)"))

        w2_grouped = []
        w2_c = []
        w2_s = []

        def round_w2(b):
            grouped = ring.tile([P, N * PACK], BF16, name="w2_grouped", align_bytes=64)
            interleave(grouped[:], w2_raw[b][:])
            w2_grouped.append(grouped)

        def quantize_w2(b):
            codes = keep.tile([P, N], U32, name=f"w2_c{b}", tag=w2_tags[b], align_bytes=64)
            scales = keep.tile([P, N], U8, name=f"w2_s{b}", align_bytes=64)
            quantize(codes[:], scales[:], w2_grouped[b][:])
            w2_c.append(codes)
            w2_s.append(scales)

        first_bank = {(0, W4): 6, (0, W2): 4, (1, W4): 0, (1, W2): 2}
        scores = {}

        def open_scores(half):
            for kind in (W4, W2):
                for pair in range(2):
                    number = first_bank[half, kind] + pair
                    scores[half, kind, pair] = bank(number, [P, 2, HALF], F32, f"y{half}{kind}{pair}")

        def second_pass(half, b):
            cols = slice(half * HALF, (half + 1) * HALF)
            for pair in range(2):
                for kind in (W4, W2):
                    for i in range(2):
                        nb = 2 * pair + i
                        if kind == W4:
                            codes = w4_w[:, b, 2 * P * nb : 2 * P * (nb + 1)].bitcast(FP4X4)
                            scales = w4_s[:, b, P * nb : P * (nb + 1)]
                        else:
                            codes = w2_c[b][:, P * nb : P * (nb + 1)].bitcast(FP8X4)
                            scales = w2_s[b][:, P * nb : P * (nb + 1)]
                        nc.tensor.matmul_mx(
                            out=scores[half, kind, pair][:, i, :],
                            lhsT=codes,
                            lhsT_scale=scales,
                            rhs=x_c[b][:, cols].bitcast(FP8X4),
                            rhs_scale=x_s[b][:, cols],
                            start=(b == 0 and i == 0),
                            stop=(b == R_PASSES - 1 and i == 1),
                        )

        def scores_out(half):
            for pair in range(2):
                y4 = ring.tile([P, 2, HALF], F32, name="y4")
                result = ring.tile([P, 2, HALF], F32, name="result", bufs=4)
                for i in range(2):
                    nb = 2 * pair + i
                    nc.scalar.activation(
                        out=y4[:, i, :],
                        in_=scores[half, W4, pair][:, i, :],
                        func=ACT.Identity,
                        bias=bias_cols[:, nb : nb + 1],
                    )
                    nc.vector.scalar_tensor_tensor(
                        out=result[:, i, :],
                        in0=scores[half, W2, pair][:, i, :],
                        scalar=bias_cols[:, nb : nb + 1],
                        in1=y4[:, i, :],
                        op0=ALU.add,
                        op1=ALU.min,
                    )
                    target = out[nb * P : (nb + 1) * P, half * HALF : (half + 1) * HALF]
                    nc.sync.dma_start(out=target, in_=result[:, i, :])

        round_w1(0)
        quantize_w1(0)
        first_product(0)
        fetch_old(0)
        cap_and_weigh(0)
        for s in range(LO):
            put_new(s)
            round_w1(s + 1)
            quantize_w1(s + 1)
            first_product(s + 1)
            fetch_old(s + 1)
            fetch_new(s, 0, PICK)
            cap_and_weigh(s + 1)
            make_x(s, 0, PICK)
        for s in range(LO + 1, LAST + 1):
            round_w1(s)
        for b in range(R_PASSES):
            round_w2(b)
        quantize_w1(LO + 1)
        first_product(LO + 1)
        cap_and_weigh(LO + 1)
        for two in range(LO // 2):
            turn_lo(two)
        regroup_lo()
        for s in range(LO, LAST):
            put_new(s)
            fetch_old(s + 1)
            fetch_new(s, 0, PICK)
            if s > LO:
                cap_and_weigh(s + 1)
            if s + 2 <= LAST:
                quantize_w1(s + 2)
                first_product(s + 2)
            make_x(s, 0, PICK)
            if s + 2 == LAST:
                quantize_w2(0)
        put_new(LAST)
        quantize_x(0, 0, PICK)
        for half in range(2):
            open_scores(half)
            second_pass(half, 0)
        fetch_new(LAST, 0, HALF)
        fetch_new(LAST, HALF, PICK)
        make_x(LAST, 0, HALF)
        regroup_hi(nc.scalar.copy, 0, HALF)
        make_x(LAST, HALF, PICK)
        regroup_hi(nc.vector.tensor_copy, HALF, PICK)
        quantize_x(1, 0, HALF)
        quantize_w2(1)
        second_pass(0, 1)
        quantize_x(1, HALF, PICK)
        second_pass(1, 1)
        for half in range(2):
            scores_out(half)
